import numpy as np
import ml_dtypes


def mxq(x, axis, fmt="e4m3"):
    dtype, down = {"e4m3": (ml_dtypes.float8_e4m3fn, 7), "e5m2": (ml_dtypes.float8_e5m2, 14)}[fmt]
    v = np.moveaxis(np.asarray(x, np.float32).astype(ml_dtypes.bfloat16).astype(np.float64), axis, -1)
    blocks = v.reshape(v.shape[:-1] + (-1, 32))
    amax = np.abs(blocks).max(-1, keepdims=True)
    byte = np.maximum(np.where(amax > 0, np.frexp(amax)[1] - 1 + 127, 0) - down, 1)
    scale = np.exp2(byte - 127.0)
    codes = (blocks / scale).astype(np.float32).astype(dtype).astype(np.float64)
    return np.moveaxis((codes * scale).reshape(v.shape), -1, axis)


WIDE = False


def mx_kscale(k):
    if not WIDE:
        return np.ones(k)
    levels = np.array([10, -10, 5, -5, 0])
    if k % 512:
        return np.exp2(np.random.permutation(np.resize(levels, k // 32))).repeat(32)
    a = np.empty((k // 512, 16))
    for p in range(k // 512):
        a[p, :8] = np.random.permutation(np.resize(levels, 8))
        for g in range(8):
            far = levels[np.abs(levels - a[p, g]) >= 10]
            a[p, g + 8] = far[np.random.randint(len(far))]
    return np.exp2(a.ravel()).repeat(32)


BF16 = ml_dtypes.bfloat16


def bf(x):
    return np.asarray(x, np.float32).astype(BF16)


def f64(x):
    return np.asarray(x).astype(np.float64)


E2M1 = np.array([0.0, 0.5, 1.0, 1.5, 2.0, 3.0, 4.0, 6.0, -0.0, -0.5, -1.0, -1.5, -2.0, -3.0, -4.0, -6.0])


def pack_weight(w, fmt):
    k, n = w.shape
    w = f64(bf(w)).reshape(k // 32, 32, n)
    amax = np.abs(w).max(1)
    if fmt == "e4m3":
        byte = np.frexp(amax)[1] - 1 + 127 - 7
    else:
        mant, ex = np.frexp(amax / 6.0)
        byte = np.where(mant > 0.5, ex, ex - 1) + 127
    byte = np.clip(np.where(amax > 0, byte, 1), 1, 254)
    scaled = (w * np.exp2(127.0 - byte)[:, None, :]).reshape(k, n).astype(np.float32)
    by_word = np.ascontiguousarray(scaled.reshape(k // 512, 128, 4, n).transpose(0, 1, 3, 2))
    if fmt == "e4m3":
        words = by_word.astype(ml_dtypes.float8_e4m3fn).view(np.uint8)
    else:
        c = by_word.astype(ml_dtypes.float4_e2m1fn).view(np.uint8) & 0xF
        words = c[..., 0::2] | (c[..., 1::2] << 4)
    return np.ascontiguousarray(words), np.ascontiguousarray(byte.astype(np.uint8).reshape(k // 512, 16, n))


def unpack_weight(words, scales, fmt):
    g, p, n, _ = words.shape
    if fmt == "e4m3":
        vals = np.ascontiguousarray(words).view(ml_dtypes.float8_e4m3fn).astype(np.float64)
    else:
        nib = np.empty((g, p, n, 4), np.uint8)
        nib[..., 0::2] = words & 0xF
        nib[..., 1::2] = words >> 4
        vals = E2M1[nib]
    vals = vals * np.repeat(np.exp2(scales.astype(np.float64) - 127.0), 8, axis=1)[..., None]
    return vals.transpose(0, 1, 3, 2).reshape(g * 512, n)
def pack4(w):
    words, scales = pack_weight(w, "e2m1")
    return words.reshape(words.shape[0], 128, -1), scales


def unpack4(words, scales):
    return unpack_weight(words.reshape(words.shape[0], 128, -1, 2), scales, "e2m1")


S, F, C, D = 2048, 1024, 512, 2048


def draw0():
    s, t = mx_kscale(F), mx_kscale(S)
    x = np.random.standard_normal((S, F)) * s
    w = 0.7 * np.random.standard_normal((F, C)) / np.sqrt(F) / s[:, None]
    base = 0.3 * np.random.standard_normal(C)
    ratio = np.exp(0.2 * np.random.standard_normal(S)) * t
    eps_words, eps_scales = pack4(np.random.standard_normal((S, D)) / np.sqrt(S) / t[:, None])
    return {"x": bf(x), "w": bf(w), "base": bf(base), "ratio": bf(ratio),
            "eps_words": eps_words, "eps_scales": eps_scales}


def core(x, w, base, ratio, eps_words, eps_scales):
    cost = mxq(f64(x), 1, "e4m3") @ mxq(f64(w), 0, "e4m3")
    weight = np.exp(f64(base) - cost) * f64(ratio)[:, None]
    eps = unpack4(eps_words, eps_scales)
    return mxq(weight, 0, "e4m3").T @ eps


def e4m3fn_bytes(y):
    return np.clip(np.asarray(y, np.float64), -448.0, 448.0).astype(np.float32).astype(ml_dtypes.float8_e4m3fn).view(np.uint8)


def e4m3fn_values(b):
    return np.asarray(b, np.uint8).view(ml_dtypes.float8_e4m3fn).astype(np.float64)


def setup_inputs():
    d = draw0()
    x0 = np.asarray(d['x']).astype(np.float64)
    s = (np.max(np.abs(x0), axis=(0,), keepdims=True) / 448.0).astype(np.float32)
    out = {}
    for k, v in d.items():
        if k == 'x':
            out['x_bytes'] = e4m3fn_bytes(x0 / s.astype(np.float64))
            out['x_scale'] = s
        else:
            out[k] = v
    return out


def reference(x_bytes, x_scale, w, base, ratio, eps_words, eps_scales):
    return core(e4m3fn_values(x_bytes) * x_scale.astype(np.float64), w, base, ratio, eps_words, eps_scales)

from contextlib import ExitStack

import concourse.mybir as mybir
from concourse.masks import make_identity

F32 = mybir.dt.float32
BF16 = mybir.dt.bfloat16
U32 = mybir.dt.uint32
I32 = mybir.dt.int32
U8 = mybir.dt.uint8
FP8 = mybir.dt.float8_e4m3fn
FP8X4 = mybir.dt.float8_e4m3fn_x4
FP4X4 = mybir.dt.float4_e2m1fn_x4
ALU = mybir.AluOpType
ACT = mybir.ActivationFunctionType

P = 128
S, F, C, D = 2048, 1024, 512, 2048
KP = 512
NG = S // KP
NQ = F // KP
NT = 4
NC = C // P
NB = 512
ND = D // NB

POOLX = ((1, 3),)
VMUL = ((2, 2), (2, 3), (3, 0), (3, 1), (3, 2), (3, 3))
IW = ("pool", "scalar")
FLOPS = 2 * S * F * C + 2 * C * S * D


def tile_mppi_control_update_s13_kernel(tc, x_bytes, x_scale, w, base, ratio, eps_words, eps_scales, out):
    nc = tc.nc
    with ExitStack() as ctx:
        sb = ctx.enter_context(tc.tile_pool(name="sb", bufs=1))
        psum = ctx.enter_context(tc.psum_pool(name="psum", bufs=1))
        ctx.enter_context(tc.manual_schedule())

        def buf(tag, bufs, shape, dtype):
            return sb.tile(shape, dtype, name=tag, tag=tag, bufs=bufs, align_bytes=64)

        def bank(tag, shape):
            return psum.tile(shape, F32, name=tag, tag=tag)

        e_plane = buf("e_plane", 1, [P, NG, D], U8)
        nc.vector.memset(e_plane[:].rearrange("p g n -> p (g n)").bitcast(I32), 0)
        warm = buf("warm", 1, [P, 1], F32)
        warm_out = buf("warm_out", 1, [P, 1], F32)
        nc.vector.memset(warm[:], 0.0)

        xs = buf("xs", 1, [P, NQ, 4], F32)
        nc.scalar.dma_start(out=xs[:], in_=x_scale.rearrange("o (q p t) -> p (o q) t", p=P, t=4))
        base_bf = buf("base_bf", 1, [P, NC], BF16)
        nc.scalar.dma_start(out=base_bf[:], in_=base.rearrange("(p t) -> p t", t=NC))
        nc.scalar.activation(out=warm_out[:], in_=warm[:], func=ACT.Exp)

        ident = buf("ident", 1, [P, P], F32)
        make_identity(nc, ident[:])

        x_rows = x_bytes.rearrange("(g p t) k -> g p t k", p=P, t=NT)
        xb = [buf("xb", NG, [P, NT, F], U8) for g in range(NG)]
        w_rows = w.rearrange("(q p j) c -> q p j c", p=P, j=4)
        w_raw = [buf("w_raw", NQ, [P, 4, C], BF16) for q in range(NQ)]
        for h in (0, 2):
            nc.sync.dma_start(out=xb[0][:, h : h + 2, :], in_=x_rows[0][:, h : h + 2, :])
        xs_bc = buf("xs_bc", 1, [P, KP], F32)
        nc.sync.dma_start(out=xs_bc[:], in_=x_scale.rearrange("o k -> (o k)")[KP:].partition_broadcast(P))
        for q in range(NQ):
            nc.sync.dma_start(out=w_raw[q][:], in_=w_rows[q])
        for g in range(1, NG):
            nc.sync.dma_start(out=xb[g][:], in_=x_rows[g])
        ratio_bc = buf("ratio_bc", 1, [P, S], BF16)
        nc.sync.dma_start(out=ratio_bc[:], in_=ratio.partition_broadcast(P))
        e_rows = eps_scales.bitcast(I32).rearrange("g q n -> q g n")
        for quad in range(4):
            nc.sync.dma_start(
                out=e_plane[32 * quad : 32 * quad + 4, :, :].bitcast(I32), in_=e_rows[4 * quad : 4 * quad + 4]
            )
        e_words = [buf("e_words", NG, [P, 2 * D], U8) for g in range(NG)]
        for g in range(NG):
            nc.sync.dma_start(out=e_words[g][:], in_=eps_words[g])

        base_f = buf("base_f", 1, [P, NC], F32)
        nc.vector.tensor_copy(out=base_f[:], in_=base_bf[:])

        w_grouped, w_codes, w_scales = [], [], []
        for q in range(NQ):
            w_grouped.append(buf("w_grouped", NQ, [P, C, 4], BF16))
            w_codes.append(buf("w_codes", NQ, [P, C], U32))
            w_scales.append(buf("w_scales", NQ, [P, C], U8))

        def interleave_w(q, cts):
            engine = IW[q]
            dst = w_grouped[q][:].rearrange("p (t m) j -> p t m j", t=NC)
            src = w_raw[q][:].rearrange("p j (m t) -> p t m j", t=NC)
            for ct in cts:
                if engine == "pool":
                    nc.gpsimd.tensor_scalar(
                        out=dst[:, ct], in0=src[:, ct], scalar1=1.0, scalar2=0.0, op0=ALU.mult, op1=ALU.add
                    )
                elif engine == "scalar":
                    nc.scalar.copy(out=dst[:, ct], in_=src[:, ct])
                else:
                    nc.vector.tensor_copy(out=dst[:, ct], in_=src[:, ct])

        def quantise_w(q, half):
            cols = slice(256 * half, 256 * (half + 1))
            nc.vector.quantize_mx(
                out=w_codes[q][:, cols].bitcast(FP8X4),
                scales=w_scales[q][:, cols],
                in_=w_grouped[q][:, cols, :].rearrange("p c j -> p (c j)"),
            )

        xp = {}
        xf, xt, xg, x_codes, x_scales = {}, {}, {}, {}, {}
        cost, ex, eb, wt, wg = {}, {}, {}, {}, {}
        m_codes = buf("m_codes", 1, [P, NG, C], U32)
        m_scales = buf("m_scales", 1, [P, NG, C], U8)

        def cast(g, t, part=slice(0, F)):
            if (g, t) not in xf:
                xf[g, t] = buf("xf", 8, [P, F], BF16)
            nc.scalar.copy(out=xf[g, t][:, part], in_=xb[g][:, t, part].bitcast(FP8))

        def prescale_x(g, n, a):
            if a == 0:
                xp[g, n] = buf("xp", 3, [P, 2, 2, 2 * P], BF16)
            if True:
                nc.gpsimd.tensor_tensor(
                    out=xp[g, n][:, a].rearrange("p u (i e) -> p u i e", e=2),
                    in0=xf[g, n - 1 + a][:, KP:].rearrange("p (i u e) -> p u i e", u=2, e=2),
                    in1=xs_bc[:].rearrange("p (i u e) -> p u i e", u=2, e=2),
                    op=ALU.mult,
                )

        def turn_x(g, n):
            h, q = divmod(n, NQ)
            if n == 0:
                for i in range(NQ):
                    xg[g, i] = buf("xg", 2 * NQ, [P, KP, 4], BF16)
            xt[g, n] = bank("xt%d" % (n % 2), [P, 2, 2 * P])
            for a in range(2):
                for u in range(2):
                    if (g, n) in POOLX:
                        src = xp[g, n][:, a, u].bitcast(F32)
                    else:
                        src = xf[g, 2 * h + a][:].bitcast(F32)[:, 256 * q + u : 256 * (q + 1) : 2]
                    nc.tensor.transpose(xt[g, n][:, u, P * a : P * (a + 1)], src, ident[:])

        def scale_x(g, n):
            h, q = divmod(n, NQ)
            rows = slice(2 * P * h, 2 * P * (h + 1))
            if (g, n) in POOLX:
                nc.scalar.copy(
                    out=xg[g, q][:, rows, :].bitcast(F32), in_=xt[g, n][:].rearrange("p u r -> p r u")
                )
            else:
                nc.vector.tensor_tensor(
                    out=xg[g, q][:, rows, :].rearrange("p r (u e) -> p r u e", u=2),
                    in0=xt[g, n][:].bitcast(BF16).rearrange("p u (r e) -> p r u e", e=2),
                    in1=xs[:, q : q + 1, :].rearrange("p q (u e) -> p q u e", u=2).to_broadcast([P, 2 * P, 2, 2]),
                    op=ALU.mult,
                )

        def quantise_x(g, q):
            x_codes[g, q] = buf("x_codes", 2 * NQ, [P, KP], U32)
            x_scales[g, q] = buf("x_scales", 2 * NQ, [P, KP], U8)
            nc.vector.quantize_mx(
                out=x_codes[g, q][:].bitcast(FP8X4),
                scales=x_scales[g, q][:],
                in_=xg[g, q][:].rearrange("p r j -> p (r j)"),
            )

        def product1(g, ct):
            cost[g, ct] = bank("cost%d" % (ct % 2), [P, KP])
            cols = slice(P * ct, P * (ct + 1))
            for q in range(NQ):
                nc.tensor.matmul_mx(
                    out=cost[g, ct][:],
                    lhsT=w_codes[q][:, cols].bitcast(FP8X4),
                    lhsT_scale=w_scales[q][:, cols],
                    rhs=x_codes[g, q][:].bitcast(FP8X4),
                    rhs_scale=x_scales[g, q][:],
                    start=(q == 0),
                    stop=(q == NQ - 1),
                )

        def exponential(g, ct):
            ex[g, ct] = buf("ex", 6, [P, KP], F32)
            nc.scalar.activation(
                out=ex[g, ct][:], in_=cost[g, ct][:], func=ACT.Exp, bias=base_f[:, ct : ct + 1], scale=-1.0
            )

        def times_ratio(g, ct):
            engine = nc.vector if (g, ct) in VMUL else nc.gpsimd
            eb[g, ct] = buf("eb", 8, [P, 2, 256], BF16)
            engine.tensor_tensor(
                out=eb[g, ct][:].rearrange("p u (i e) -> p u i e", e=2),
                in0=ex[g, ct][:].rearrange("p (u e i) -> p u i e", u=2, e=2),
                in1=ratio_bc[:, KP * g : KP * (g + 1)].rearrange("p (i u e) -> p u i e", u=2, e=2),
                op=ALU.mult,
            )

        def turn_m(g, pair, tag):
            wt[g, pair] = bank(tag, [P, 2, 2, P])
            for a in range(2):
                for u in range(2):
                    nc.tensor.transpose(
                        wt[g, pair][:, a, u, :], eb[g, 2 * pair + a][:, u, :].bitcast(F32), ident[:]
                    )

        def empty_m(g, pair):
            if pair == 0:
                wg[g] = buf("wg", 2, [P, C, 4], BF16)
            nc.scalar.copy(
                out=wg[g][:, 256 * pair : 256 * (pair + 1), :].bitcast(F32).rearrange("p (a c) u -> p a c u", a=2),
                in_=wt[g, pair][:].rearrange("p a u c -> p a c u"),
            )

        def quantise_m(g, pair):
            cols = slice(256 * pair, 256 * (pair + 1))
            nc.vector.quantize_mx(
                out=m_codes[:, g, cols].bitcast(FP8X4),
                scales=m_scales[:, g, cols],
                in_=wg[g][:, cols, :].rearrange("p c j -> p (c j)"),
            )

        acc = {}

        def product2(o, g, tag):
            ct, dt = divmod(o, ND)
            if g == 0:
                acc[o] = bank(tag, [P, NB])
            cols = slice(P * ct, P * (ct + 1))
            nc.tensor.matmul_mx(
                out=acc[o][:],
                lhsT=m_codes[:, g, cols].bitcast(FP8X4),
                lhsT_scale=m_scales[:, g, cols],
                rhs=e_words[g][:, 2 * NB * dt : 2 * NB * (dt + 1)].bitcast(FP4X4),
                rhs_scale=e_plane[:, g, NB * dt : NB * (dt + 1)],
                start=(g == 0),
                stop=(g == NG - 1),
            )

        out_rows = out.rearrange("(p t) d -> t p d", t=NC)

        def finish(o):
            ct, dt = divmod(o, ND)
            res = buf("res", 16, [P, NB], F32)
            if o % 2 == 0:
                nc.vector.tensor_copy(out=res[:], in_=acc[o][:])
            else:
                nc.scalar.copy(out=res[:], in_=acc[o][:])
            nc.sync.dma_start(out=out_rows[ct][:, NB * dt : NB * (dt + 1)], in_=res[:])

        HELD = {0: "acc0", 1: "acc1", 2: "acc2"}

        def chain(g, ct):
            product1(g, ct)
            exponential(g, ct)

        for t in range(NT):
            cast(0, t)
        interleave_w(0, (0, 1, 2, 3))
        interleave_w(1, (0, 1, 2, 3))

        for n in range(4):
            turn_x(0, n)
            scale_x(0, n)
        for t in range(NT):
            cast(1, t)
        quantise_x(0, 0)
        quantise_x(0, 1)
        for s in range(1, NG):
            for n in (1, 3):
                if (s, n) in POOLX:
                    prescale_x(s, n, 0)
                    prescale_x(s, n, 1)
            turn_x(s, 0)
            turn_x(s, 1)
            if s >= 2:
                turn_m(s - 2, 0, "wt")
            scale_x(s, 0)
            if s == 1:
                for q in range(NQ):
                    quantise_w(q, 0)
                    quantise_w(q, 1)
            scale_x(s, 1)
            chain(s - 1, 0)
            if s >= 2:
                empty_m(s - 2, 0)
            chain(s - 1, 1)
            times_ratio(s - 1, 0)
            times_ratio(s - 1, 1)
            if s + 1 < NG:
                cast(s + 1, 0)
                cast(s + 1, 1)
            turn_x(s, 2)
            turn_x(s, 3)
            if s >= 2:
                turn_m(s - 2, 1, "wt")
                empty_m(s - 2, 1)
            scale_x(s, 2)
            scale_x(s, 3)
            chain(s - 1, 2)
            chain(s - 1, 3)
            if s + 1 < NG:
                cast(s + 1, 2)
                cast(s + 1, 3)
            times_ratio(s - 1, 2)
            times_ratio(s - 1, 3)
            if s >= 2:
                quantise_m(s - 2, 0)
            quantise_x(s, 0)
            if s >= 2:
                quantise_m(s - 2, 1)
            quantise_x(s, 1)
            if s >= 2:
                for o in HELD:
                    product2(o, s - 2, HELD[o])

        last = NG - 1
        chain(last, 0)
        chain(last, 1)
        turn_m(last - 1, 0, "xt0")
        empty_m(last - 1, 0)
        turn_m(last - 1, 1, "xt1")
        empty_m(last - 1, 1)
        times_ratio(last, 0)
        chain(last, 2)
        chain(last, 3)
        times_ratio(last, 1)
        quantise_m(last - 1, 0)
        quantise_m(last - 1, 1)
        times_ratio(last, 2)
        times_ratio(last, 3)
        tail = ("wt", "cost0", "cost1", "xt0", "xt1", "acc0", "acc1", "acc2", "wt", "cost0", "cost1", "xt0", "xt1")
        product2(3, 0, "wt")
        product2(3, 1, "wt")
        for o in HELD:
            product2(o, last - 1, HELD[o])
        product2(3, last - 1, "wt")
        turn_m(last, 0, "xt0")
        empty_m(last, 0)
        turn_m(last, 1, "xt1")
        quantise_m(last, 0)
        empty_m(last, 1)
        quantise_m(last, 1)
        for o in (4, 5):
            for g in range(last):
                product2(o, g, tail[o - 3])
        for o in range(6):
            product2(o, last, "")
            finish(o)
        for o in range(6, NC * ND):
            for g in range(NG):
                product2(o, g, tail[o - 3])
            finish(o)
